import numpy as np
CORES = [30,6,62,38,9,49,17,41]
N = 8
W, H, TIMES = 512, 1, 1
WTS = [1,2,1]
def setup_inputs(rng):
    return {"x": rng.standard_normal((N, 128, W), dtype=np.float32)}
def reference(x):
    g = np.concatenate(list(x.astype(np.float64)), axis=1)
    for _ in range(TIMES):
        p = np.concatenate([g[:, -H:], g, g[:, :H]], axis=1)
        g = sum(WTS[i] * p[:, i:i + N * W] for i in range(2 * H + 1))
    return {"y": np.stack([g[:, W * r:W * r + W] for r in range(N)]).astype(np.float32 if x.dtype != np.float64 else np.float64)}

from concourse.bass import DstId, RemoteDMATransfer
from concourse.mybir import AluOpType

NCH = 4
_W = 512

SCRATCH = {
    "e0": ("dram", [128, 2], "float32"),
    "e1": ("dram", [128, 2], "float32"),
    "rbuf": ("dram", [128, 2], "float32"),
    "hl": ("sbuf", [128, 4], "float32"),
    "hr": ("sbuf", [128, 4], "float32"),
    "P": ("sbuf", [128, 4], "float32"),
    "X": ("sbuf", [128, _W], "float32"),
    "S": ("sbuf", [128, _W], "float32"),
    "Y": ("sbuf", [128, _W], "float32"),
}
SEMAPHORES = (["ed0", "ed1", "rin", "arrL", "arrR", "sent", "stored", "p", "yl", "yr"]
              + ["ld%d" % k for k in range(NCH)] + ["s%d" % k for k in range(NCH)] + ["y%d" % k for k in range(NCH)])


def _hops(topo, a, b):
    ca, cb = topo.chip(a), topo.chip(b)
    if ca == cb:
        return 0
    if topo.mates(ca, cb) or topo.same_plane(ca, cb):
        return 1
    return 2


def _engines(mask, n, skip=0):
    bits = [b for b in range(mask.bit_length()) if (mask >> b) & 1]
    return sum(1 << b for b in bits[skip:skip + n])


def _count(mask):
    return sum((mask >> b) & 1 for b in range(mask.bit_length()))


def _plan(T, topo):
    cores = list(T.cores)
    n = len(cores)
    chips = set(topo.chip(c) for c in cores)
    free = [c for c in range(topo.CORES_PER_CHIP * topo.CHIPS) if topo.chip(c) in chips and c not in cores]
    plan = []
    for r in range(n):
        for side, d in ((0, (r - 1) % n), (1, (r + 1) % n)):
            src, dst = cores[r], cores[d]
            relay = None
            if not topo.may_write(src, dst):
                cands = [c for c in free if topo.may_write(src, c) and topo.may_write(c, dst)]
                relay = min(cands, key=lambda c: (
                    _hops(topo, src, c) + _hops(topo, c, dst), _hops(topo, c, dst),
                    (topo.die(src) != topo.die(c)) + (topo.die(c) != topo.die(dst)), c))
                free.remove(relay)
            plan.append((r, d, side, relay))
    return plan


def _land(T, side):
    if side == 0:
        return T.hr[:, 0:2], T.sem.arrR
    return T.hl[:, 0:2], T.sem.arrL


def rank_program(g, core, T, topo):
    plan = _plan(T, topo)
    cores = list(T.cores)

    for (r, d, side, relay) in plan:
        if relay == core:
            dst = cores[d]
            out, sem = _land(T, side)
            rid, pid, _ = topo.addr(dst)
            m = topo.mask(core, dst)
            g.wait_ge(T.sem.rin, 1)
            g.remote_dma(out_ap=out, in_ap=T.rbuf[:], remote_sem=sem, local_sem=T.sem.sent,
                         pid=pid, routing_id=rid, dma_engine_mask=m)
            g.wait_ge(T.sem.sent, _count(m))

    rank = T.rank_of(core)
    if rank is None:
        return

    w = list(T.tables["WTS"])
    if w != [1, 2, 1]:
        raise ValueError("the pair-sum form is for the weights [1, 2, 1]")
    W = T.x.shape[1]
    add = AluOpType.add
    q = [g.sync, g.scalar]
    v = g.vector
    cb = [W * k // NCH for k in range(NCH + 1)]

    g.sync.dma_start(T.e0[:], T.x[:, 0:2]).then_inc(T.sem.ed0, 16)
    g.scalar.dma_start(T.e1[:], T.x[:, W - 2:W]).then_inc(T.sem.ed1, 16)
    for k in range(NCH):
        q[k % 2].dma_start(T.X[:, cb[k]:cb[k + 1]], T.x[:, cb[k]:cb[k + 1]]).then_inc(T.sem["ld%d" % k], 16)

    edge = [T.e0, T.e1]
    edsem = [T.sem.ed0, T.sem.ed1]
    sends = sorted([p for p in plan if p[0] == rank], key=lambda p: p[3] is None)
    sent = 0
    if all(p[3] is not None for p in sends):
        trs = []
        for j, (r, d, side, relay) in enumerate(sends):
            g.wait_ge(edsem[side], 16)
            rid, pid, _ = topo.addr(relay)
            trs.append(RemoteDMATransfer(dst_ids=[DstId(rid=rid, pnc=pid)],
                                         dma_engine_mask=_engines(topo.mask(core, relay), 1, j),
                                         remote_sem=T.sem.rin, src=edge[side][:], dst=T.rbuf[:]))
            sent += 1
        g.remote_dma_fused(trs, local_sem=T.sem.sent)
    else:
        for (r, d, side, relay) in sends:
            g.wait_ge(edsem[side], 16)
            if relay is not None:
                rid, pid, _ = topo.addr(relay)
                m = _engines(topo.mask(core, relay), 1)
                out, sem = T.rbuf[:], T.sem.rin
            else:
                rid, pid, _ = topo.addr(cores[d])
                m = topo.mask(core, cores[d])
                out, sem = _land(T, side)
            g.remote_dma(out_ap=out, in_ap=edge[side][:], remote_sem=sem, local_sem=T.sem.sent,
                         pid=pid, routing_id=rid, dma_engine_mask=m)
            sent += _count(m)

    stores = 0
    for k in range(NCH):
        lo, hi = max(0, cb[k] - 1), cb[k + 1] - 1
        v.wait_ge(T.sem["ld%d" % k], 16)
        v.tensor_tensor(T.S[:, lo:hi], T.X[:, lo:hi], T.X[:, lo + 1:hi + 1], add).then_inc(T.sem["s%d" % k], 1)
        lo = max(1, lo)
        v.wait_ge(T.sem["s%d" % k], 1)
        v.tensor_tensor(T.Y[:, lo:hi], T.S[:, lo - 1:hi - 1], T.S[:, lo:hi], add).then_inc(T.sem["y%d" % k], 1)
        lo, hi = max(2, lo), min(W - 2, hi)
        q[k % 2].wait_ge(T.sem["y%d" % k], 1)
        q[k % 2].dma_start(T.y[:, lo:hi], T.Y[:, lo:hi]).then_inc(T.sem.stored, 16)
        stores += 1

    v.tensor_tensor(T.P[:, 0:1], T.X[:, 0:1], T.S[:, 0:1], add).then_inc(T.sem.p, 1)
    v.tensor_tensor(T.P[:, 1:2], T.X[:, W - 1:W], T.S[:, W - 2:W - 1], add).then_inc(T.sem.p, 1)
    v.wait_ge(T.sem.p, 2)

    n = len(cores)
    left_relayed = [p[3] for p in plan if p[1] == rank and p[2] == 1][0] is not None
    right_relayed = [p[3] for p in plan if p[1] == rank and p[2] == 0][0] is not None
    arr_n = {}
    for (r, d, side, relay) in plan:
        if d == rank:
            arr_n[side] = _count(topo.mask(cores[r] if relay is None else relay, core))
    order = sorted([(left_relayed, 0), (right_relayed, 1)])
    qa, qb = q[0], q[(NCH - 1) % 2]
    for (_, s) in order:
        if s == 0:
            v.wait_ge(T.sem.arrL, arr_n[1])
            v.tensor_tensor(T.Y[:, 0:1], T.P[:, 0:1], T.hl[:, 1:2], add).then_inc(T.sem.yl, 1)
            qa.wait_ge(T.sem.yl, 1)
            qa.dma_start(T.y[:, 0:2], T.Y[:, 0:2]).then_inc(T.sem.stored, 16)
        else:
            v.wait_ge(T.sem.arrR, arr_n[0])
            v.tensor_tensor(T.Y[:, W - 1:W], T.P[:, 1:2], T.hr[:, 0:1], add).then_inc(T.sem.yr, 1)
            qb.wait_ge(T.sem.yr, 1)
            qb.dma_start(T.y[:, W - 2:W], T.Y[:, W - 2:W]).then_inc(T.sem.stored, 16)
        stores += 1

    g.wait_ge(T.sem.sent, sent)
    g.wait_ge(T.sem.stored, 16 * stores)
